import numpy as np
import ml_dtypes

BF16 = ml_dtypes.bfloat16


def bf(x):
    return np.asarray(x, np.float32).astype(BF16)


def f32(x):
    return np.asarray(x, np.float32)


def f64(x):
    return np.asarray(x).astype(np.float64)


def striped(idx):
    return np.tile(idx.reshape(-1, 16).T, (8, 1))


S, K, M, N, E, Q = 512, 128, 512, 128, 2, 64


def setup_inputs():
    return {"base": bf(np.random.standard_normal((M, S))), "x": bf(np.random.standard_normal((K, N))), "w": bf(np.random.standard_normal((E, K, M)) / np.sqrt(K)), "b": f32(0.5 * np.random.standard_normal((M, 1))), "offs": striped(np.random.permutation(S)[:N])}


def reference(base, x, w, b, offs):
    idx = offs[:16].T.reshape(-1)
    z = f64(base).copy()
    for e in range(E):
        z[:, idx[e * Q : (e + 1) * Q]] = f64(w)[e].T @ f64(x)[:, e * Q : (e + 1) * Q]
    return np.maximum(z + f64(b), 0.0)

@@ -1,0 +1,61 @@
+import concourse.mybir as mybir
+from concourse.masks import make_identity
+
+BF16, F32, U16 = mybir.dt.bfloat16, mybir.dt.float32, mybir.dt.uint16
+RELU = mybir.ActivationFunctionType.Relu
+
+P = 128
+FLOPS = 2 * 512 * 128 * 128
+
+
+def tile_scatter_matmul_kernel(tc, base, x, w, b, offs, out):
+    nc = tc.nc
+    M, S = base.shape
+    E, K, _ = w.shape
+    N = x.shape[1]
+    A = M // P
+    Q = N // E
+
+    with (
+        tc.tile_pool(name="held", bufs=1) as held,
+        tc.psum_pool(name="psum", bufs=1) as psum,
+    ):
+        base_t = held.tile([P, A, S], BF16, name="base_t")
+        x_t = held.tile([P, N], BF16, name="x_t")
+        w_t = held.tile([P, E, M], BF16, name="w_t")
+        b_t = held.tile([P, A], F32, name="b_t")
+        offsets = held.tile([P, N // 16], U16, name="offsets")
+        nc.sync.dma_start(base_t[:], base.rearrange("(a p) s -> p a s", p=P))
+        nc.sync.dma_start(offsets[:], offs)
+        nc.sync.dma_start(x_t[:], x)
+        nc.sync.dma_start(w_t[:], w.rearrange("e k m -> k e m"))
+        nc.sync.dma_start(b_t[:], b.rearrange("(a p) o -> p (a o)", p=P))
+
+        ident = held.tile([P, P], BF16, name="ident")
+        make_identity(nc, ident[:])
+
+        windows = [psum.tile([P, S], F32, name=f"window{a}") for a in range(A)]
+        for a in range(A):
+            nc.tensor.matmul(windows[a][:], ident[:], base_t[:, a, :], start=True, stop=True)
+
+        for a in range(A):
+            for e in range(E):
+                piece = offsets[:, e * Q // 16 : (e + 1) * Q // 16]
+                nc.tensor.matmul(
+                    windows[a][:].indirect(piece),
+                    w_t[:, e, a * P : (a + 1) * P],
+                    x_t[:, e * Q : (e + 1) * Q],
+                    start=True,
+                    stop=True,
+                )
+
+        for a in range(A):
+            result = held.tile([P, S], F32, name=f"result{a}")
+            if a % 2 == 0:
+                nc.vector.tensor_scalar(
+                    result[:], windows[a][:], b_t[:, a : a + 1], 0.0,
+                    mybir.AluOpType.add, mybir.AluOpType.max,
+                )
+            else:
+                nc.scalar.activation(result[:], windows[a][:], RELU, bias=b_t[:, a : a + 1])
+            nc.sync.dma_start(out[a * P : (a + 1) * P, :], result[:])

@@ -16,6 +16,8 @@ def tile_scatter_matmul_kernel(tc, base, x, w, b, offs, out):
     A = M // P
     Q = N // E
 
+    out_rows = out.rearrange("(p a) s -> p a s", a=A)
+
     with (
         tc.tile_pool(name="held", bufs=1) as held,
         tc.psum_pool(name="psum", bufs=1) as psum,
@@ -25,11 +27,11 @@ def tile_scatter_matmul_kernel(tc, base, x, w, b, offs, out):
         w_t = held.tile([P, E, M], BF16, name="w_t")
         b_t = held.tile([P, A], F32, name="b_t")
         offsets = held.tile([P, N // 16], U16, name="offsets")
-        nc.sync.dma_start(base_t[:], base.rearrange("(a p) s -> p a s", p=P))
+        nc.sync.dma_start(base_t[:], base.rearrange("(p a) s -> p a s", a=A))
         nc.sync.dma_start(offsets[:], offs)
         nc.sync.dma_start(x_t[:], x)
         nc.sync.dma_start(w_t[:], w.rearrange("e k m -> k e m"))
-        nc.sync.dma_start(b_t[:], b.rearrange("(a p) o -> p (a o)", p=P))
+        nc.sync.dma_start(b_t[:], b.rearrange("(p a) o -> p (a o)", a=A))
 
         ident = held.tile([P, P], BF16, name="ident")
         make_identity(nc, ident[:])
@@ -43,7 +45,7 @@ def tile_scatter_matmul_kernel(tc, base, x, w, b, offs, out):
                 piece = offsets[:, e * Q // 16 : (e + 1) * Q // 16]
                 nc.tensor.matmul(
                     windows[a][:].indirect(piece),
-                    w_t[:, e, a * P : (a + 1) * P],
+                    w_t[:, e, a::A],
                     x_t[:, e * Q : (e + 1) * Q],
                     start=True,
                     stop=True,
@@ -58,4 +60,4 @@ def tile_scatter_matmul_kernel(tc, base, x, w, b, offs, out):
                 )
             else:
                 nc.scalar.activation(result[:], windows[a][:], RELU, bias=b_t[:, a : a + 1])
-            nc.sync.dma_start(out[a * P : (a + 1) * P, :], result[:])
+            nc.sync.dma_start(out_rows[:, a, :], result[:])

@@ -5,6 +5,7 @@ BF16, F32, U16 = mybir.dt.bfloat16, mybir.dt.float32, mybir.dt.uint16
 RELU = mybir.ActivationFunctionType.Relu
 
 P = 128
+WARM_UP = 4
 FLOPS = 2 * 512 * 128 * 128
 
 
@@ -32,6 +33,16 @@ def tile_scatter_matmul_kernel(tc, base, x, w, b, offs, out):
         nc.sync.dma_start(x_t[:], x)
         nc.sync.dma_start(w_t[:], w.rearrange("e k m -> k e m"))
         nc.sync.dma_start(b_t[:], b.rearrange("(p a) o -> p (a o)", a=A))
+
+        zero = held.tile([P, 1], F32, name="zero")
+        relu_of_zero = held.tile([P, 1], F32, name="relu_of_zero")
+        zeros = held.tile([P, S], BF16, name="zeros")
+        spare = psum.tile([P, S], F32, name="spare")
+        nc.vector.memset(zero[:], 0.0)
+        nc.vector.memset(zeros[:], 0.0)
+        nc.scalar.activation(relu_of_zero[:], zero[:], RELU, bias=zero[:])
+        for i in range(WARM_UP):
+            nc.tensor.matmul(spare[:], zeros[:, :P], zeros[:], start=True, stop=True)
 
         ident = held.tile([P, P], BF16, name="ident")
         make_identity(nc, ident[:])

@@ -5,7 +5,7 @@ BF16, F32, U16 = mybir.dt.bfloat16, mybir.dt.float32, mybir.dt.uint16
 RELU = mybir.ActivationFunctionType.Relu
 
 P = 128
-WARM_UP = 4
+WARM_UP = 3
 FLOPS = 2 * 512 * 128 * 128
 
 
@@ -28,7 +28,9 @@ def tile_scatter_matmul_kernel(tc, base, x, w, b, offs, out):
         w_t = held.tile([P, E, M], BF16, name="w_t")
         b_t = held.tile([P, A], F32, name="b_t")
         offsets = held.tile([P, N // 16], U16, name="offsets")
-        nc.sync.dma_start(base_t[:], base.rearrange("(p a) s -> p a s", a=A))
+        base_rows = base.rearrange("(p a) s -> p a s", a=A)
+        for a in range(0, A, 2):
+            nc.sync.dma_start(base_t[:, a : a + 2, :], base_rows[:, a : a + 2, :])
         nc.sync.dma_start(offsets[:], offs)
         nc.sync.dma_start(x_t[:], x)
         nc.sync.dma_start(w_t[:], w.rearrange("e k m -> k e m"))
@@ -38,8 +40,8 @@ def tile_scatter_matmul_kernel(tc, base, x, w, b, offs, out):
         relu_of_zero = held.tile([P, 1], F32, name="relu_of_zero")
         zeros = held.tile([P, S], BF16, name="zeros")
         spare = psum.tile([P, S], F32, name="spare")
-        nc.vector.memset(zero[:], 0.0)
         nc.vector.memset(zeros[:], 0.0)
+        nc.vector.memset(zero[:], 0.0)
         nc.scalar.activation(relu_of_zero[:], zero[:], RELU, bias=zero[:])
         for i in range(WARM_UP):
             nc.tensor.matmul(spare[:], zeros[:, :P], zeros[:], start=True, stop=True)

@@ -64,13 +64,17 @@ def tile_scatter_matmul_kernel(tc, base, x, w, b, offs, out):
                     stop=True,
                 )
 
+        H = S // 2
         for a in range(A):
-            result = held.tile([P, S], F32, name=f"result{a}")
-            if a % 2 == 0:
-                nc.vector.tensor_scalar(
-                    result[:], windows[a][:], b_t[:, a : a + 1], 0.0,
-                    mybir.AluOpType.add, mybir.AluOpType.max,
-                )
-            else:
-                nc.scalar.activation(result[:], windows[a][:], RELU, bias=b_t[:, a : a + 1])
-            nc.sync.dma_start(out_rows[:, a, :], result[:])
+            bias = b_t[:, a : a + 1]
+            for h in range(2):
+                half = slice(h * H, (h + 1) * H)
+                result = held.tile([P, H], F32, name=f"result{a}_{h}")
+                if a % 2 == 0:
+                    nc.vector.tensor_scalar(
+                        result[:], windows[a][:, half], bias, 0.0,
+                        mybir.AluOpType.add, mybir.AluOpType.max,
+                    )
+                else:
+                    nc.scalar.activation(result[:], windows[a][:, half], RELU, bias=bias)
+                nc.sync.dma_start(out_rows[:, a, half], result[:])

import concourse.mybir as mybir
from concourse.masks import make_identity

BF16, F32, U16 = mybir.dt.bfloat16, mybir.dt.float32, mybir.dt.uint16
RELU = mybir.ActivationFunctionType.Relu

P = 128
WARM_UP = 3
FLOPS = 2 * 512 * 128 * 128


def tile_scatter_matmul_kernel(tc, base, x, w, b, offs, out):
    nc = tc.nc
    M, S = base.shape
    E, K, _ = w.shape
    N = x.shape[1]
    A = M // P
    Q = N // E

    out_rows = out.rearrange("(p a) s -> p a s", a=A)

    with (
        tc.tile_pool(name="held", bufs=1) as held,
        tc.psum_pool(name="psum", bufs=1) as psum,
    ):
        base_t = held.tile([P, A, S], BF16, name="base_t")
        x_t = held.tile([P, N], BF16, name="x_t")
        w_t = held.tile([P, E, M], BF16, name="w_t")
        b_t = held.tile([P, A], F32, name="b_t")
        offsets = held.tile([P, N // 16], U16, name="offsets")
        base_rows = base.rearrange("(p a) s -> p a s", a=A)
        for a in range(0, A, 2):
            nc.sync.dma_start(base_t[:, a : a + 2, :], base_rows[:, a : a + 2, :])
        nc.sync.dma_start(offsets[:], offs)
        nc.sync.dma_start(x_t[:], x)
        nc.sync.dma_start(w_t[:], w.rearrange("e k m -> k e m"))
        nc.sync.dma_start(b_t[:], b.rearrange("(p a) o -> p (a o)", a=A))

        zero = held.tile([P, 1], F32, name="zero")
        relu_of_zero = held.tile([P, 1], F32, name="relu_of_zero")
        zeros = held.tile([P, S], BF16, name="zeros")
        spare = psum.tile([P, S], F32, name="spare")
        nc.vector.memset(zeros[:], 0.0)
        nc.vector.memset(zero[:], 0.0)
        nc.scalar.activation(relu_of_zero[:], zero[:], RELU, bias=zero[:])
        for i in range(WARM_UP):
            nc.tensor.matmul(spare[:], zeros[:, :P], zeros[:], start=True, stop=True)

        ident = held.tile([P, P], BF16, name="ident")
        make_identity(nc, ident[:])

        windows = [psum.tile([P, S], F32, name=f"window{a}") for a in range(A)]
        for a in range(A):
            nc.tensor.matmul(windows[a][:], ident[:], base_t[:, a, :], start=True, stop=True)

        for a in range(A):
            for e in range(E):
                piece = offsets[:, e * Q // 16 : (e + 1) * Q // 16]
                nc.tensor.matmul(
                    windows[a][:].indirect(piece),
                    w_t[:, e, a::A],
                    x_t[:, e * Q : (e + 1) * Q],
                    start=True,
                    stop=True,
                )

        H = S // 2
        for a in range(A):
            bias = b_t[:, a : a + 1]
            for h in range(2):
                half = slice(h * H, (h + 1) * H)
                result = held.tile([P, H], F32, name=f"result{a}_{h}")
                if a % 2 == 0:
                    nc.vector.tensor_scalar(
                        result[:], windows[a][:, half], bias, 0.0,
                        mybir.AluOpType.add, mybir.AluOpType.max,
                    )
                else:
                    nc.scalar.activation(result[:], windows[a][:, half], RELU, bias=bias)
                nc.sync.dma_start(out_rows[:, a, half], result[:])
